import numpy as np
import ml_dtypes

BF16 = ml_dtypes.bfloat16


def bf(x):
    return np.asarray(x, np.float32).astype(BF16)


def f32(x):
    return np.asarray(x, np.float32)


def f64(x):
    return np.asarray(x).astype(np.float64)


def striped(idx):
    return np.tile(idx.reshape(-1, 16).T, (8, 1))


def rows(idx, k):
    return np.tile(idx, (k, 1))


def look(tab, idx):
    return np.take_along_axis(f64(tab), rows(idx, len(tab)), axis=1)


K, S, V, N, M = 512, 256, 256, 256, 128


def setup_inputs():
    return {"tab": f32(np.random.standard_normal((K, S))), "qry": f32(np.random.standard_normal((K, V))), "w": bf(np.random.uniform(0.0, 2.0, (K, M)) / K), "offs": striped(np.random.randint(0, S, N))}


def reference(tab, qry, w, offs):
    idx = offs[:16].T.reshape(-1)
    x = (look(tab, idx) - f64(qry)) ** 2
    y = f64(w).T @ x
    return y

@@ -1,0 +1,51 @@
+import concourse.mybir as mybir
+
+P = 128
+K, S, N, M = 512, 256, 256, 128
+BLOCKS = K // P
+PIECE = 128
+PIECES = N // PIECE
+STRIPE = 16
+
+FLOPS = 2 * K * M * N
+
+BF16, F32, U16 = mybir.dt.bfloat16, mybir.dt.float32, mybir.dt.uint16
+SUBTRACT = mybir.AluOpType.subtract
+SQUARE = mybir.ActivationFunctionType.Square
+
+
+def tile_lookup_dist_sub_none_kernel(tc, tab, qry, w, offs, out):
+    nc = tc.nc
+    tab_rows = tab.rearrange("(p b) s -> p b s", b=BLOCKS)
+    qry_rows = qry.rearrange("(p b) n -> p b n", b=BLOCKS)
+    w_rows = w.rearrange("(p b) m -> p (b m)", b=BLOCKS)
+
+    with (
+        tc.tile_pool(name="held", bufs=1) as held,
+        tc.psum_pool(name="psum", bufs=1) as psum,
+    ):
+        offsets = held.tile([P, N // STRIPE], U16, name="offsets")
+        weights = held.tile([P, BLOCKS * M], BF16, name="weights")
+        windows = [held.tile([P, S], F32, name=f"window{b}") for b in range(BLOCKS)]
+        queries = [held.tile([P, N], F32, name=f"query{b}") for b in range(BLOCKS)]
+        diffs = [held.tile([P, N], F32, name=f"diff{b}") for b in range(BLOCKS)]
+        squares = [held.tile([P, N], BF16, name=f"square{b}") for b in range(BLOCKS)]
+        result = held.tile([P, N], F32, name="result")
+        acc = psum.tile([P, N], F32, name="acc")
+
+        nc.sync.dma_start(offsets[:], offs)
+        nc.scalar.dma_start(weights[:], w_rows)
+        for b in range(BLOCKS):
+            nc.sync.dma_start(windows[b][:], tab_rows[:, b, :])
+            nc.sync.dma_start(queries[b][:], qry_rows[:, b, :])
+
+        for b in range(BLOCKS):
+            for h in range(PIECES):
+                cols = slice(h * PIECE, (h + 1) * PIECE)
+                entries = offsets[:, h * PIECE // STRIPE : (h + 1) * PIECE // STRIPE]
+                nc.vector.tensor_tensor(diffs[b][:, cols], windows[b][:].indirect(entries), queries[b][:, cols], SUBTRACT)
+            nc.scalar.activation(squares[b][:], diffs[b][:], SQUARE)
+            nc.tensor.matmul(acc[:], weights[:, b * M : (b + 1) * M], squares[b][:], start=(b == 0), stop=(b == BLOCKS - 1))
+
+        nc.vector.tensor_copy(result[:], acc[:])
+        nc.sync.dma_start(out, result[:])

@@ -28,24 +28,27 @@ def tile_lookup_dist_sub_none_kernel(tc, tab, qry, w, offs, out):
         weights = held.tile([P, BLOCKS * M], BF16, name="weights")
         windows = [held.tile([P, S], F32, name=f"window{b}") for b in range(BLOCKS)]
         queries = [held.tile([P, N], F32, name=f"query{b}") for b in range(BLOCKS)]
-        diffs = [held.tile([P, N], F32, name=f"diff{b}") for b in range(BLOCKS)]
-        squares = [held.tile([P, N], BF16, name=f"square{b}") for b in range(BLOCKS)]
         result = held.tile([P, N], F32, name="result")
-        acc = psum.tile([P, N], F32, name="acc")
+        accs = [psum.tile([P, PIECE], F32, name=f"acc{h}") for h in range(PIECES)]
 
-        nc.sync.dma_start(offsets[:], offs)
-        nc.scalar.dma_start(weights[:], w_rows)
         for b in range(BLOCKS):
             nc.sync.dma_start(windows[b][:], tab_rows[:, b, :])
             nc.sync.dma_start(queries[b][:], qry_rows[:, b, :])
+            if b == 0:
+                nc.sync.dma_start(offsets[:], offs)
+        nc.sync.dma_start(weights[:], w_rows)
 
         for b in range(BLOCKS):
             for h in range(PIECES):
                 cols = slice(h * PIECE, (h + 1) * PIECE)
                 entries = offsets[:, h * PIECE // STRIPE : (h + 1) * PIECE // STRIPE]
-                nc.vector.tensor_tensor(diffs[b][:, cols], windows[b][:].indirect(entries), queries[b][:, cols], SUBTRACT)
-            nc.scalar.activation(squares[b][:], diffs[b][:], SQUARE)
-            nc.tensor.matmul(acc[:], weights[:, b * M : (b + 1) * M], squares[b][:], start=(b == 0), stop=(b == BLOCKS - 1))
+                diff = held.tile([P, PIECE], F32, name=f"diff{b}_{h}")
+                square = held.tile([P, PIECE], BF16, name=f"square{b}_{h}")
+                nc.vector.tensor_tensor(diff[:], windows[b][:].indirect(entries), queries[b][:, cols], SUBTRACT)
+                nc.scalar.activation(square[:], diff[:], SQUARE)
+                nc.tensor.matmul(accs[h][:], weights[:, b * M : (b + 1) * M], square[:], start=(b == 0), stop=(b == BLOCKS - 1))
 
-        nc.vector.tensor_copy(result[:], acc[:])
-        nc.sync.dma_start(out, result[:])
+        nc.scalar.copy(result[:, :PIECE], accs[0][:])
+        nc.sync.dma_start(out[:, :PIECE], result[:, :PIECE])
+        nc.vector.tensor_copy(result[:, PIECE:], accs[1][:])
+        nc.sync.dma_start(out[:, PIECE:], result[:, PIECE:])

@@ -5,6 +5,8 @@ K, S, N, M = 512, 256, 256, 128
 BLOCKS = K // P
 PIECE = 128
 PIECES = N // PIECE
+WARM_COLS = 512
+WARM_MATMULS = 8
 STRIPE = 16
 
 FLOPS = 2 * K * M * N
@@ -37,6 +39,12 @@ def tile_lookup_dist_sub_none_kernel(tc, tab, qry, w, offs, out):
             if b == 0:
                 nc.sync.dma_start(offsets[:], offs)
         nc.sync.dma_start(weights[:], w_rows)
+
+        zeros = held.tile([P, WARM_COLS], BF16, name="zeros")
+        scratch = psum.tile([P, WARM_COLS], F32, name="scratch")
+        nc.vector.memset(zeros[:], 0.0)
+        for step in range(WARM_MATMULS):
+            nc.tensor.matmul(scratch[:], zeros[:, :M], zeros[:], start=(step == 0), stop=(step == WARM_MATMULS - 1))
 
         for b in range(BLOCKS):
             for h in range(PIECES):

import concourse.mybir as mybir

P = 128
K, S, N, M = 512, 256, 256, 128
BLOCKS = K // P
PIECE = 128
PIECES = N // PIECE
WARM_COLS = 512
WARM_MATMULS = 8
STRIPE = 16

FLOPS = 2 * K * M * N

BF16, F32, U16 = mybir.dt.bfloat16, mybir.dt.float32, mybir.dt.uint16
SUBTRACT = mybir.AluOpType.subtract
SQUARE = mybir.ActivationFunctionType.Square


def tile_lookup_dist_sub_none_kernel(tc, tab, qry, w, offs, out):
    nc = tc.nc
    tab_rows = tab.rearrange("(p b) s -> p b s", b=BLOCKS)
    qry_rows = qry.rearrange("(p b) n -> p b n", b=BLOCKS)
    w_rows = w.rearrange("(p b) m -> p (b m)", b=BLOCKS)

    with (
        tc.tile_pool(name="held", bufs=1) as held,
        tc.psum_pool(name="psum", bufs=1) as psum,
    ):
        offsets = held.tile([P, N // STRIPE], U16, name="offsets")
        weights = held.tile([P, BLOCKS * M], BF16, name="weights")
        windows = [held.tile([P, S], F32, name=f"window{b}") for b in range(BLOCKS)]
        queries = [held.tile([P, N], F32, name=f"query{b}") for b in range(BLOCKS)]
        result = held.tile([P, N], F32, name="result")
        accs = [psum.tile([P, PIECE], F32, name=f"acc{h}") for h in range(PIECES)]

        for b in range(BLOCKS):
            nc.sync.dma_start(windows[b][:], tab_rows[:, b, :])
            nc.sync.dma_start(queries[b][:], qry_rows[:, b, :])
            if b == 0:
                nc.sync.dma_start(offsets[:], offs)
        nc.sync.dma_start(weights[:], w_rows)

        zeros = held.tile([P, WARM_COLS], BF16, name="zeros")
        scratch = psum.tile([P, WARM_COLS], F32, name="scratch")
        nc.vector.memset(zeros[:], 0.0)
        for step in range(WARM_MATMULS):
            nc.tensor.matmul(scratch[:], zeros[:, :M], zeros[:], start=(step == 0), stop=(step == WARM_MATMULS - 1))

        for b in range(BLOCKS):
            for h in range(PIECES):
                cols = slice(h * PIECE, (h + 1) * PIECE)
                entries = offsets[:, h * PIECE // STRIPE : (h + 1) * PIECE // STRIPE]
                diff = held.tile([P, PIECE], F32, name=f"diff{b}_{h}")
                square = held.tile([P, PIECE], BF16, name=f"square{b}_{h}")
                nc.vector.tensor_tensor(diff[:], windows[b][:].indirect(entries), queries[b][:, cols], SUBTRACT)
                nc.scalar.activation(square[:], diff[:], SQUARE)
                nc.tensor.matmul(accs[h][:], weights[:, b * M : (b + 1) * M], square[:], start=(b == 0), stop=(b == BLOCKS - 1))

        nc.scalar.copy(result[:, :PIECE], accs[0][:])
        nc.sync.dma_start(out[:, :PIECE], result[:, :PIECE])
        nc.vector.tensor_copy(result[:, PIECE:], accs[1][:])
        nc.sync.dma_start(out[:, PIECE:], result[:, PIECE:])
